import numpy as np
import ml_dtypes


def mxq(x, axis, fmt="e4m3"):
    dtype, down = {"e4m3": (ml_dtypes.float8_e4m3fn, 7), "e5m2": (ml_dtypes.float8_e5m2, 14)}[fmt]
    v = np.moveaxis(np.asarray(x, np.float32).astype(ml_dtypes.bfloat16).astype(np.float64), axis, -1)
    blocks = v.reshape(v.shape[:-1] + (-1, 32))
    amax = np.abs(blocks).max(-1, keepdims=True)
    byte = np.maximum(np.where(amax > 0, np.frexp(amax)[1] - 1 + 127, 0) - down, 1)
    scale = np.exp2(byte - 127.0)
    codes = (blocks / scale).astype(np.float32).astype(dtype).astype(np.float64)
    return np.moveaxis((codes * scale).reshape(v.shape), -1, axis)


WIDE = False


def mx_kscale(k):
    if not WIDE:
        return np.ones(k)
    levels = np.array([10, -10, 5, -5, 0])
    if k % 512:
        return np.exp2(np.random.permutation(np.resize(levels, k // 32))).repeat(32)
    a = np.empty((k // 512, 16))
    for p in range(k // 512):
        a[p, :8] = np.random.permutation(np.resize(levels, 8))
        for g in range(8):
            far = levels[np.abs(levels - a[p, g]) >= 10]
            a[p, g + 8] = far[np.random.randint(len(far))]
    return np.exp2(a.ravel()).repeat(32)


def f64(x):
    return np.asarray(x).astype(np.float64)


def striped(idx):
    return np.tile(idx.reshape(-1, 16).T, (8, 1)).astype(np.uint16)


def unstriped(offs):
    return offs[:16].T.reshape(-1).astype(np.int64)


E2M1 = np.array([0.0, 0.5, 1.0, 1.5, 2.0, 3.0, 4.0, 6.0, -0.0, -0.5, -1.0, -1.5, -2.0, -3.0, -4.0, -6.0])


def pack_weight(w, fmt):
    k, n = w.shape
    w = f64(np.asarray(w, np.float32).astype(ml_dtypes.bfloat16)).reshape(k // 32, 32, n)
    amax = np.abs(w).max(1)
    if fmt == "e4m3":
        byte = np.frexp(amax)[1] - 1 + 127 - 7
    else:
        mant, ex = np.frexp(amax / 6.0)
        byte = np.where(mant > 0.5, ex, ex - 1) + 127
    byte = np.clip(np.where(amax > 0, byte, 1), 1, 254)
    scaled = (w * np.exp2(127.0 - byte)[:, None, :]).reshape(k, n).astype(np.float32)
    by_word = np.ascontiguousarray(scaled.reshape(k // 512, 128, 4, n).transpose(0, 1, 3, 2))
    if fmt == "e4m3":
        words = by_word.astype(ml_dtypes.float8_e4m3fn).view(np.uint8)
    else:
        c = by_word.astype(ml_dtypes.float4_e2m1fn).view(np.uint8) & 0xF
        words = (c[..., 0::2] | (c[..., 1::2] << 4)).reshape(k // 512, 128, 2 * n)
    return np.ascontiguousarray(words), np.ascontiguousarray(byte.astype(np.uint8).reshape(k // 512, 16, n))


def unpack_weight(words, scales, fmt):
    g, _, n = scales.shape
    words = np.ascontiguousarray(words).reshape(g, 128, n, -1)
    if fmt == "e4m3":
        vals = words.view(ml_dtypes.float8_e4m3fn).astype(np.float64)
    else:
        nib = np.empty((g, 128, n, 4), np.uint8)
        nib[..., 0::2] = words & 0xF
        nib[..., 1::2] = words >> 4
        vals = E2M1[nib]
    vals = vals * np.repeat(np.exp2(scales.astype(np.float64) - 127.0), 8, axis=1)[..., None]
    return vals.transpose(0, 1, 3, 2).reshape(g * 512, n)


def split(x):
    m, e = np.frexp(f64(x))
    hi = np.ldexp(np.trunc(16.0 * m) / 16.0, e)
    return hi, f64(x) - hi


K, M, T, S = 512, 128, 2048, 1024


def setup_inputs():
    n = np.random.standard_normal
    s = mx_kscale(K)[:, None]
    v = pack_weight(n((K, T)) * s, "e4m3")
    return {
        "tab_words": v[0],
        "tab_scales": v[1],
        "w": (n((K, M)) / np.sqrt(K) / s).astype(np.float32),
        "gT": n((M, T)).astype(np.float32),
        "offs": striped(np.random.permutation(T)[:S]),
    }


def reference(tab_words, tab_scales, w, gT, offs):
    tab_ = unpack_weight(tab_words, tab_scales, "e4m3")[:, unstriped(offs)]
    w_hi, w_lo = split(w)
    w_hi_, w_lo_ = mxq(w_hi, 0, "e4m3"), mxq(w_lo, 0, "e4m3")
    y = w_hi_.T @ tab_ + w_lo_.T @ tab_
    return (y) * f64(gT)[:, unstriped(offs)]

@@ -1,0 +1,149 @@
+from contextlib import ExitStack
+
+import concourse.mybir as mybir
+
+K, M, T, S = 512, 128, 2048, 1024
+FLOPS = 2 * 2 * K * M * S
+
+F32 = mybir.dt.float32
+BF16 = mybir.dt.bfloat16
+I32 = mybir.dt.int32
+U32 = mybir.dt.uint32
+U16 = mybir.dt.uint16
+U8 = mybir.dt.uint8
+FP8X4 = mybir.dt.float8_e4m3fn_x4
+ALU = mybir.AluOpType
+
+P = 128
+PACK = 4
+GROUP = 16
+HI_MASK = -(1 << 20)
+
+SCALE_CUTS = [512,512]
+WORD_CUTS = [256,256,256,256]
+MM_CUTS = [256,256,256,256]
+GATE_CUTS = [256,256,256,128,128]
+
+
+def spans(widths):
+    starts = [sum(widths[:i]) for i in range(len(widths))]
+    return [(a, a + n) for a, n in zip(starts, widths)]
+
+
+def tile_list_tabgate_none_kernel(tc, tab_words, tab_scales, w, gT, offs, out):
+    nc = tc.nc
+    with ExitStack() as ctx:
+        keep = ctx.enter_context(tc.tile_pool(name="keep", bufs=1))
+        psum = ctx.enter_context(tc.psum_pool(name="psum", bufs=1))
+
+        offsets = keep.tile([P, S // GROUP], U16, name="offsets")
+        w_raw = keep.tile([P, PACK, M], F32, name="w_raw")
+        scale_table = keep.tile([P, T // 4], I32, name="scale_table", align_bytes=64)
+        word_table = keep.tile([P, T], I32, name="word_table", align_bytes=64)
+        gate_table = keep.tile([P, T], F32, name="gate_table", align_bytes=64)
+        w_lo = keep.tile([P, PACK, M], BF16, name="w_lo", align_bytes=64)
+        w_hi = keep.tile([P, PACK, M], I32, name="w_hi", align_bytes=64)
+        w_parts = keep.tile([P, 2, M * PACK], BF16, name="w_parts", align_bytes=64)
+        w_codes = keep.tile([P, 2 * M], U32, name="w_codes", align_bytes=64)
+        w_scales = keep.tile([P, 2 * M], U8, name="w_scales", align_bytes=64)
+        v_codes = keep.tile([P, S], U32, name="v_codes", align_bytes=64)
+        v_scales = keep.tile([P, S], U8, name="v_scales", align_bytes=64)
+        y = keep.tile([P, S], F32, name="y", align_bytes=64)
+        gated = keep.tile([P, S], F32, name="gated", align_bytes=64)
+
+        def listed(a, b):
+            return offsets[:, a // GROUP : b // GROUP]
+
+        def load_w(j0, j1):
+            nc.sync.dma_start(out=w_raw[:, j0:j1, :], in_=w.rearrange("(p j) n -> p j n", j=PACK)[:, j0:j1, :])
+
+        def load_scales():
+            scale_rows = tab_scales[0].bitcast(I32)
+            for r in range(4):
+                nc.sync.dma_start(out=scale_table[r:P:32, :], in_=scale_rows[r:16:4, :])
+
+        def load_words():
+            nc.sync.dma_start(out=word_table[:], in_=tab_words[0].rearrange("p t i -> p (t i)").bitcast(I32))
+
+        def load_gates():
+            nc.sync.dma_start(out=gate_table[:], in_=gT)
+
+        def split_hi(j0, j1):
+            nc.vector.tensor_scalar(
+                out=w_hi[:, j0:j1, :], in0=w_raw[:, j0:j1, :].bitcast(I32),
+                scalar1=HI_MASK, scalar2=None, op0=ALU.bitwise_and,
+            )
+
+        def split_lo(j0, j1):
+            nc.vector.tensor_tensor(
+                out=w_lo[:, j0:j1, :], in0=w_raw[:, j0:j1, :], in1=w_hi[:, j0:j1, :].bitcast(F32), op=ALU.subtract,
+            )
+
+        def weave_hi():
+            nc.scalar.copy(
+                out=w_parts[:, 0, :].rearrange("p (n j) -> p n j", j=PACK),
+                in_=w_hi[:].bitcast(F32).rearrange("p j n -> p n j"),
+            )
+
+        def weave_lo():
+            nc.scalar.copy(
+                out=w_parts[:, 1, :].rearrange("p (n j) -> p n j", j=PACK),
+                in_=w_lo[:].rearrange("p j n -> p n j"),
+            )
+
+        def quantize_w():
+            nc.vector.quantize_mx(
+                out=w_codes[:].bitcast(FP8X4), scales=w_scales[:],
+                in_=w_parts[:].rearrange("p h c -> p (h c)"),
+            )
+
+        def gather_scales(i):
+            a, b = spans(SCALE_CUTS)[i]
+            nc.vector.tensor_copy(v_scales[:, a:b], scale_table[:].bitcast(U8).indirect(listed(a, b)))
+
+        def gather_words(i):
+            a, b = spans(WORD_CUTS)[i]
+            nc.vector.tensor_copy(v_codes[:, a:b], word_table[:].bitcast(U32).indirect(listed(a, b)))
+
+        def project(i):
+            a, b = spans(MM_CUTS)[i]
+            acc = psum.tile([M, b - a], F32, name="acc%d" % i)
+            for h in range(2):
+                nc.tensor.matmul_mx(
+                    out=acc[:],
+                    lhsT=w_codes[:, h * M : (h + 1) * M].bitcast(FP8X4),
+                    lhsT_scale=w_scales[:, h * M : (h + 1) * M],
+                    rhs=v_codes[:, a:b].bitcast(FP8X4),
+                    rhs_scale=v_scales[:, a:b],
+                    start=(h == 0),
+                    stop=(h == 1),
+                )
+            nc.scalar.copy(out=y[:, a:b], in_=acc[:])
+
+        def gate(i):
+            a, b = spans(GATE_CUTS)[i]
+            nc.vector.tensor_tensor(gated[:, a:b], gate_table[:].indirect(listed(a, b)), y[:, a:b], ALU.mult)
+            nc.sync.dma_start(out=out[:, a:b], in_=gated[:, a:b])
+
+        nc.vector.memset(scale_table[:], 0)
+        load_w(0, 2)
+        load_w(2, 4)
+        nc.sync.dma_start(offsets[:], offs)
+        load_scales()
+        load_words()
+        load_gates()
+        split_hi(0, 2)
+        split_hi(2, 4)
+        split_lo(0, 2)
+        split_lo(2, 4)
+        weave_hi()
+        weave_lo()
+        gather_scales(0)
+        gather_scales(1)
+        quantize_w()
+        for i in range(len(WORD_CUTS)):
+            gather_words(i)
+        for i in range(len(MM_CUTS)):
+            project(i)
+        for i in range(len(GATE_CUTS)):
+            gate(i)

@@ -19,7 +19,8 @@ PACK = 4
 GROUP = 16
 HI_MASK = -(1 << 20)
 
-SCALE_CUTS = [512,512]
+EARLY = 256
+SCALE_CUTS = [1024]
 WORD_CUTS = [256,256,256,256]
 MM_CUTS = [256,256,256,256]
 GATE_CUTS = [256,256,256,128,128]
@@ -41,12 +42,12 @@ def tile_list_tabgate_none_kernel(tc, tab_words, tab_scales, w, gT, offs, out):
         scale_table = keep.tile([P, T // 4], I32, name="scale_table", align_bytes=64)
         word_table = keep.tile([P, T], I32, name="word_table", align_bytes=64)
         gate_table = keep.tile([P, T], F32, name="gate_table", align_bytes=64)
-        w_lo = keep.tile([P, PACK, M], BF16, name="w_lo", align_bytes=64)
+        w_lo = keep.tile([P, PACK, M], BF16, name="w_lo", tag="lo_then_codes", align_bytes=64)
         w_hi = keep.tile([P, PACK, M], I32, name="w_hi", align_bytes=64)
         w_parts = keep.tile([P, 2, M * PACK], BF16, name="w_parts", align_bytes=64)
         w_codes = keep.tile([P, 2 * M], U32, name="w_codes", align_bytes=64)
         w_scales = keep.tile([P, 2 * M], U8, name="w_scales", align_bytes=64)
-        v_codes = keep.tile([P, S], U32, name="v_codes", align_bytes=64)
+        codes_early = keep.tile([P, EARLY], U32, name="codes_early", align_bytes=64)
         v_scales = keep.tile([P, S], U8, name="v_scales", align_bytes=64)
         y = keep.tile([P, S], F32, name="y", align_bytes=64)
         gated = keep.tile([P, S], F32, name="gated", align_bytes=64)
@@ -75,7 +76,7 @@ def tile_list_tabgate_none_kernel(tc, tab_words, tab_scales, w, gT, offs, out):
             )
 
         def split_lo(j0, j1):
-            nc.vector.tensor_tensor(
+            nc.gpsimd.tensor_tensor(
                 out=w_lo[:, j0:j1, :], in0=w_raw[:, j0:j1, :], in1=w_hi[:, j0:j1, :].bitcast(F32), op=ALU.subtract,
             )
 
@@ -103,7 +104,7 @@ def tile_list_tabgate_none_kernel(tc, tab_words, tab_scales, w, gT, offs, out):
 
         def gather_words(i):
             a, b = spans(WORD_CUTS)[i]
-            nc.vector.tensor_copy(v_codes[:, a:b], word_table[:].bitcast(U32).indirect(listed(a, b)))
+            nc.vector.tensor_copy(v_codes(a, b), word_table[:].bitcast(U32).indirect(listed(a, b)))
 
         def project(i):
             a, b = spans(MM_CUTS)[i]
@@ -113,7 +114,7 @@ def tile_list_tabgate_none_kernel(tc, tab_words, tab_scales, w, gT, offs, out):
                     out=acc[:],
                     lhsT=w_codes[:, h * M : (h + 1) * M].bitcast(FP8X4),
                     lhsT_scale=w_scales[:, h * M : (h + 1) * M],
-                    rhs=v_codes[:, a:b].bitcast(FP8X4),
+                    rhs=v_codes(a, b).bitcast(FP8X4),
                     rhs_scale=v_scales[:, a:b],
                     start=(h == 0),
                     stop=(h == 1),
@@ -126,21 +127,22 @@ def tile_list_tabgate_none_kernel(tc, tab_words, tab_scales, w, gT, offs, out):
             nc.sync.dma_start(out=out[:, a:b], in_=gated[:, a:b])
 
         nc.vector.memset(scale_table[:], 0)
-        load_w(0, 2)
-        load_w(2, 4)
+        load_w(0, 4)
         nc.sync.dma_start(offsets[:], offs)
         load_scales()
         load_words()
         load_gates()
-        split_hi(0, 2)
-        split_hi(2, 4)
-        split_lo(0, 2)
-        split_lo(2, 4)
+        split_hi(0, 4)
+        split_lo(0, 4)
         weave_hi()
         weave_lo()
         gather_scales(0)
-        gather_scales(1)
         quantize_w()
+        codes_late = keep.tile([P, S - EARLY], U32, name="codes_late", tag="lo_then_codes", align_bytes=64)
+
+        def v_codes(a, b):
+            return codes_early[:, a:b] if b <= EARLY else codes_late[:, a - EARLY : b - EARLY]
+
         for i in range(len(WORD_CUTS)):
             gather_words(i)
         for i in range(len(MM_CUTS)):

@@ -64,7 +64,9 @@ def tile_list_tabgate_none_kernel(tc, tab_words, tab_scales, w, gT, offs, out):
                 nc.sync.dma_start(out=scale_table[r:P:32, :], in_=scale_rows[r:16:4, :])
 
         def load_words():
-            nc.sync.dma_start(out=word_table[:], in_=tab_words[0].rearrange("p t i -> p (t i)").bitcast(I32))
+            words = tab_words[0].rearrange("p t i -> p (t i)").bitcast(I32)
+            for a, b in spans([T // 2, T // 2]):
+                nc.sync.dma_start(out=word_table[:, a:b], in_=words[:, a:b])
 
         def load_gates():
             nc.sync.dma_start(out=gate_table[:], in_=gT)

@@ -38,15 +38,14 @@ def tile_list_tabgate_none_kernel(tc, tab_words, tab_scales, w, gT, offs, out):
         psum = ctx.enter_context(tc.psum_pool(name="psum", bufs=1))
 
         offsets = keep.tile([P, S // GROUP], U16, name="offsets")
-        w_raw = keep.tile([P, PACK, M], F32, name="w_raw")
+        w_raw = keep.tile([P, PACK, M], F32, name="w_raw", tag="raw_then_hi", align_bytes=64)
         scale_table = keep.tile([P, T // 4], I32, name="scale_table", align_bytes=64)
         word_table = keep.tile([P, T], I32, name="word_table", align_bytes=64)
         gate_table = keep.tile([P, T], F32, name="gate_table", align_bytes=64)
         w_lo = keep.tile([P, PACK, M], BF16, name="w_lo", tag="lo_then_codes", align_bytes=64)
         w_hi = keep.tile([P, PACK, M], I32, name="w_hi", align_bytes=64)
-        w_parts = keep.tile([P, 2, M * PACK], BF16, name="w_parts", align_bytes=64)
-        w_codes = keep.tile([P, 2 * M], U32, name="w_codes", align_bytes=64)
-        w_scales = keep.tile([P, 2 * M], U8, name="w_scales", align_bytes=64)
+        w_parts = [keep.tile([P, M * PACK], BF16, name="w_part%d" % h, align_bytes=64) for h in range(2)]
+        w_codes = [keep.tile([P, M], U32, name="w_codes%d" % h, align_bytes=64) for h in range(2)]
         codes_early = keep.tile([P, EARLY], U32, name="codes_early", align_bytes=64)
         v_scales = keep.tile([P, S], U8, name="v_scales", align_bytes=64)
         y = keep.tile([P, S], F32, name="y", align_bytes=64)
@@ -69,7 +68,8 @@ def tile_list_tabgate_none_kernel(tc, tab_words, tab_scales, w, gT, offs, out):
                 nc.sync.dma_start(out=word_table[:, a:b], in_=words[:, a:b])
 
         def load_gates():
-            nc.sync.dma_start(out=gate_table[:], in_=gT)
+            for a, b in spans([T // 2, T // 4, T // 4]):
+                nc.sync.dma_start(out=gate_table[:, a:b], in_=gT[:, a:b])
 
         def split_hi(j0, j1):
             nc.vector.tensor_scalar(
@@ -84,20 +84,20 @@ def tile_list_tabgate_none_kernel(tc, tab_words, tab_scales, w, gT, offs, out):
 
         def weave_hi():
             nc.scalar.copy(
-                out=w_parts[:, 0, :].rearrange("p (n j) -> p n j", j=PACK),
+                out=w_parts[0][:].rearrange("p (n j) -> p n j", j=PACK),
                 in_=w_hi[:].bitcast(F32).rearrange("p j n -> p n j"),
             )
 
         def weave_lo():
             nc.scalar.copy(
-                out=w_parts[:, 1, :].rearrange("p (n j) -> p n j", j=PACK),
+                out=w_parts[1][:].rearrange("p (n j) -> p n j", j=PACK),
                 in_=w_lo[:].rearrange("p j n -> p n j"),
             )
 
-        def quantize_w():
+        def quantize_w(h):
             nc.vector.quantize_mx(
-                out=w_codes[:].bitcast(FP8X4), scales=w_scales[:],
-                in_=w_parts[:].rearrange("p h c -> p (h c)"),
+                out=w_codes[h][:].bitcast(FP8X4), scales=w_scales[h][:],
+                in_=w_parts[h][:],
             )
 
         def gather_scales(i):
@@ -114,8 +114,8 @@ def tile_list_tabgate_none_kernel(tc, tab_words, tab_scales, w, gT, offs, out):
             for h in range(2):
                 nc.tensor.matmul_mx(
                     out=acc[:],
-                    lhsT=w_codes[:, h * M : (h + 1) * M].bitcast(FP8X4),
-                    lhsT_scale=w_scales[:, h * M : (h + 1) * M],
+                    lhsT=w_codes[h][:].bitcast(FP8X4),
+                    lhsT_scale=w_scales[h][:],
                     rhs=v_codes(a, b).bitcast(FP8X4),
                     rhs_scale=v_scales[:, a:b],
                     start=(h == 0),
@@ -139,7 +139,12 @@ def tile_list_tabgate_none_kernel(tc, tab_words, tab_scales, w, gT, offs, out):
         weave_hi()
         weave_lo()
         gather_scales(0)
-        quantize_w()
+        w_scales = [
+            keep.tile([P, M], U8, name="hi_scales", tag="raw_then_hi", align_bytes=64),
+            keep.tile([P, M], U8, name="lo_scales", align_bytes=64),
+        ]
+        quantize_w(0)
+        quantize_w(1)
         codes_late = keep.tile([P, S - EARLY], U32, name="codes_late", tag="lo_then_codes", align_bytes=64)
 
         def v_codes(a, b):

@@ -17,13 +17,14 @@ ALU = mybir.AluOpType
 P = 128
 PACK = 4
 GROUP = 16
+QUADRANT = 32
 HI_MASK = -(1 << 20)
+HI, LO = 0, 1
 
-EARLY = 256
-SCALE_CUTS = [1024]
-WORD_CUTS = [256,256,256,256]
-MM_CUTS = [256,256,256,256]
-GATE_CUTS = [256,256,256,128,128]
+PIECE = 256
+GATE_CUTS = [PIECE, PIECE, PIECE, PIECE // 2, PIECE // 2]
+WORD_LOADS = [T // 2, T // 2]
+GATE_LOADS = [T // 2, T // 4, T // 4]
 
 
 def spans(widths):
@@ -38,15 +39,14 @@ def tile_list_tabgate_none_kernel(tc, tab_words, tab_scales, w, gT, offs, out):
         psum = ctx.enter_context(tc.psum_pool(name="psum", bufs=1))
 
         offsets = keep.tile([P, S // GROUP], U16, name="offsets")
-        w_raw = keep.tile([P, PACK, M], F32, name="w_raw", tag="raw_then_hi", align_bytes=64)
         scale_table = keep.tile([P, T // 4], I32, name="scale_table", align_bytes=64)
         word_table = keep.tile([P, T], I32, name="word_table", align_bytes=64)
         gate_table = keep.tile([P, T], F32, name="gate_table", align_bytes=64)
-        w_lo = keep.tile([P, PACK, M], BF16, name="w_lo", tag="lo_then_codes", align_bytes=64)
-        w_hi = keep.tile([P, PACK, M], I32, name="w_hi", align_bytes=64)
-        w_parts = [keep.tile([P, M * PACK], BF16, name="w_part%d" % h, align_bytes=64) for h in range(2)]
-        w_codes = [keep.tile([P, M], U32, name="w_codes%d" % h, align_bytes=64) for h in range(2)]
-        codes_early = keep.tile([P, EARLY], U32, name="codes_early", align_bytes=64)
+        w_raw = keep.tile([P, PACK, M], F32, name="w_raw", tag="raw_buffer", align_bytes=64)
+        w_hi = keep.tile([P, PACK, M], I32, name="w_hi", tag="hi_buffer", align_bytes=64)
+        w_lo = keep.tile([P, PACK, M], BF16, name="w_lo", tag="lo_buffer", align_bytes=64)
+        w_woven = [keep.tile([P, M, PACK], BF16, name="w_woven%d" % h, align_bytes=64) for h in (HI, LO)]
+        w_codes = [keep.tile([P, M], U32, name="w_codes%d" % h, align_bytes=64) for h in (HI, LO)]
         v_scales = keep.tile([P, S], U8, name="v_scales", align_bytes=64)
         y = keep.tile([P, S], F32, name="y", align_bytes=64)
         gated = keep.tile([P, S], F32, name="gated", align_bytes=64)
@@ -54,105 +54,67 @@ def tile_list_tabgate_none_kernel(tc, tab_words, tab_scales, w, gT, offs, out):
         def listed(a, b):
             return offsets[:, a // GROUP : b // GROUP]
 
-        def load_w(j0, j1):
-            nc.sync.dma_start(out=w_raw[:, j0:j1, :], in_=w.rearrange("(p j) n -> p j n", j=PACK)[:, j0:j1, :])
+        nc.vector.memset(scale_table[:], 0)
+        nc.sync.dma_start(out=w_raw[:], in_=w.rearrange("(p i) n -> p i n", i=PACK))
+        nc.sync.dma_start(offsets[:], offs)
+        scale_rows = tab_scales[0].bitcast(I32)
+        for r in range(4):
+            nc.sync.dma_start(out=scale_table[r:P:QUADRANT, :], in_=scale_rows[r:16:4, :])
+        words = tab_words[0].rearrange("p t i -> p (t i)").bitcast(I32)
+        for a, b in spans(WORD_LOADS):
+            nc.sync.dma_start(out=word_table[:, a:b], in_=words[:, a:b])
+        for a, b in spans(GATE_LOADS):
+            nc.sync.dma_start(out=gate_table[:, a:b], in_=gT[:, a:b])
 
-        def load_scales():
-            scale_rows = tab_scales[0].bitcast(I32)
-            for r in range(4):
-                nc.sync.dma_start(out=scale_table[r:P:32, :], in_=scale_rows[r:16:4, :])
+        nc.vector.tensor_scalar(
+            out=w_hi[:], in0=w_raw[:].bitcast(I32), scalar1=HI_MASK, scalar2=None, op0=ALU.bitwise_and,
+        )
+        nc.gpsimd.tensor_tensor(out=w_lo[:], in0=w_raw[:], in1=w_hi[:].bitcast(F32), op=ALU.subtract)
+        nc.scalar.copy(out=w_woven[HI][:], in_=w_hi[:].bitcast(F32).rearrange("p i n -> p n i"))
+        nc.scalar.copy(out=w_woven[LO][:], in_=w_lo[:].rearrange("p i n -> p n i"))
 
-        def load_words():
-            words = tab_words[0].rearrange("p t i -> p (t i)").bitcast(I32)
-            for a, b in spans([T // 2, T // 2]):
-                nc.sync.dma_start(out=word_table[:, a:b], in_=words[:, a:b])
+        nc.vector.tensor_copy(v_scales[:], scale_table[:].bitcast(U8).indirect(listed(0, S)))
 
-        def load_gates():
-            for a, b in spans([T // 2, T // 4, T // 4]):
-                nc.sync.dma_start(out=gate_table[:, a:b], in_=gT[:, a:b])
+        w_scales = [
+            keep.tile([P, M], U8, name="hi_scales", tag="hi_buffer", align_bytes=64),
+            keep.tile([P, M], U8, name="lo_scales", align_bytes=64),
+        ]
+        codes_first = keep.tile([P, PIECE], U32, name="codes_first", tag="raw_buffer", align_bytes=64)
+        codes_rest = keep.tile([P, S - PIECE], U32, name="codes_rest", tag="lo_buffer", align_bytes=64)
 
-        def split_hi(j0, j1):
-            nc.vector.tensor_scalar(
-                out=w_hi[:, j0:j1, :], in0=w_raw[:, j0:j1, :].bitcast(I32),
-                scalar1=HI_MASK, scalar2=None, op0=ALU.bitwise_and,
-            )
-
-        def split_lo(j0, j1):
-            nc.gpsimd.tensor_tensor(
-                out=w_lo[:, j0:j1, :], in0=w_raw[:, j0:j1, :], in1=w_hi[:, j0:j1, :].bitcast(F32), op=ALU.subtract,
-            )
-
-        def weave_hi():
-            nc.scalar.copy(
-                out=w_parts[0][:].rearrange("p (n j) -> p n j", j=PACK),
-                in_=w_hi[:].bitcast(F32).rearrange("p j n -> p n j"),
-            )
-
-        def weave_lo():
-            nc.scalar.copy(
-                out=w_parts[1][:].rearrange("p (n j) -> p n j", j=PACK),
-                in_=w_lo[:].rearrange("p j n -> p n j"),
-            )
+        def v_codes(a, b):
+            return codes_first[:, a:b] if b <= PIECE else codes_rest[:, a - PIECE : b - PIECE]
 
         def quantize_w(h):
             nc.vector.quantize_mx(
                 out=w_codes[h][:].bitcast(FP8X4), scales=w_scales[h][:],
-                in_=w_parts[h][:],
+                in_=w_woven[h][:].rearrange("p n i -> p (n i)"),
             )
 
-        def gather_scales(i):
-            a, b = spans(SCALE_CUTS)[i]
-            nc.vector.tensor_copy(v_scales[:, a:b], scale_table[:].bitcast(U8).indirect(listed(a, b)))
-
-        def gather_words(i):
-            a, b = spans(WORD_CUTS)[i]
+        def gather_words(a, b):
             nc.vector.tensor_copy(v_codes(a, b), word_table[:].bitcast(U32).indirect(listed(a, b)))
 
-        def project(i):
-            a, b = spans(MM_CUTS)[i]
-            acc = psum.tile([M, b - a], F32, name="acc%d" % i)
-            for h in range(2):
+        pieces = spans([PIECE] * (S // PIECE))
+        quantize_w(HI)
+        gather_words(*pieces[0])
+        quantize_w(LO)
+        for a, b in pieces[1:]:
+            gather_words(a, b)
+
+        for a, b in pieces:
+            acc = psum.tile([M, PIECE], F32, name="acc%d" % (a // PIECE))
+            for h in (HI, LO):
                 nc.tensor.matmul_mx(
                     out=acc[:],
                     lhsT=w_codes[h][:].bitcast(FP8X4),
                     lhsT_scale=w_scales[h][:],
                     rhs=v_codes(a, b).bitcast(FP8X4),
                     rhs_scale=v_scales[:, a:b],
-                    start=(h == 0),
-                    stop=(h == 1),
+                    start=(h == HI),
+                    stop=(h == LO),
                 )
             nc.scalar.copy(out=y[:, a:b], in_=acc[:])
 
-        def gate(i):
-            a, b = spans(GATE_CUTS)[i]
+        for a, b in spans(GATE_CUTS):
             nc.vector.tensor_tensor(gated[:, a:b], gate_table[:].indirect(listed(a, b)), y[:, a:b], ALU.mult)
             nc.sync.dma_start(out=out[:, a:b], in_=gated[:, a:b])
-
-        nc.vector.memset(scale_table[:], 0)
-        load_w(0, 4)
-        nc.sync.dma_start(offsets[:], offs)
-        load_scales()
-        load_words()
-        load_gates()
-        split_hi(0, 4)
-        split_lo(0, 4)
-        weave_hi()
-        weave_lo()
-        gather_scales(0)
-        w_scales = [
-            keep.tile([P, M], U8, name="hi_scales", tag="raw_then_hi", align_bytes=64),
-            keep.tile([P, M], U8, name="lo_scales", align_bytes=64),
-        ]
-        quantize_w(0)
-        quantize_w(1)
-        codes_late = keep.tile([P, S - EARLY], U32, name="codes_late", tag="lo_then_codes", align_bytes=64)
-
-        def v_codes(a, b):
-            return codes_early[:, a:b] if b <= EARLY else codes_late[:, a - EARLY : b - EARLY]
-
-        for i in range(len(WORD_CUTS)):
-            gather_words(i)
-        for i in range(len(MM_CUTS)):
-            project(i)
-        for i in range(len(GATE_CUTS)):
-            gate(i)

@@ -20,6 +20,7 @@ GROUP = 16
 QUADRANT = 32
 HI_MASK = -(1 << 20)
 HI, LO = 0, 1
+LINE = 4
 
 PIECE = 256
 GATE_CUTS = [PIECE, PIECE, PIECE, PIECE // 2, PIECE // 2]
@@ -43,10 +44,10 @@ def tile_list_tabgate_none_kernel(tc, tab_words, tab_scales, w, gT, offs, out):
         word_table = keep.tile([P, T], I32, name="word_table", align_bytes=64)
         gate_table = keep.tile([P, T], F32, name="gate_table", align_bytes=64)
         w_raw = keep.tile([P, PACK, M], F32, name="w_raw", tag="raw_buffer", align_bytes=64)
-        w_hi = keep.tile([P, PACK, M], I32, name="w_hi", tag="hi_buffer", align_bytes=64)
-        w_lo = keep.tile([P, PACK, M], BF16, name="w_lo", tag="lo_buffer", align_bytes=64)
-        w_woven = [keep.tile([P, M, PACK], BF16, name="w_woven%d" % h, align_bytes=64) for h in (HI, LO)]
-        w_codes = [keep.tile([P, M], U32, name="w_codes%d" % h, align_bytes=64) for h in (HI, LO)]
+        w_hi = keep.tile([P, PACK, M], I32, name="w_hi", align_bytes=64)
+        w_woven = keep.tile([P, 2, M * PACK], BF16, name="w_woven", align_bytes=64)
+        w_codes = keep.tile([P, 2, M], U32, name="w_codes", align_bytes=64)
+        w_scales = keep.tile([P, 2, M], U8, name="w_scales", align_bytes=64)
         v_scales = keep.tile([P, S], U8, name="v_scales", align_bytes=64)
         y = keep.tile([P, S], F32, name="y", align_bytes=64)
         gated = keep.tile([P, S], F32, name="gated", align_bytes=64)
@@ -69,46 +70,37 @@ def tile_list_tabgate_none_kernel(tc, tab_words, tab_scales, w, gT, offs, out):
         nc.vector.tensor_scalar(
             out=w_hi[:], in0=w_raw[:].bitcast(I32), scalar1=HI_MASK, scalar2=None, op0=ALU.bitwise_and,
         )
-        nc.gpsimd.tensor_tensor(out=w_lo[:], in0=w_raw[:], in1=w_hi[:].bitcast(F32), op=ALU.subtract)
-        nc.scalar.copy(out=w_woven[HI][:], in_=w_hi[:].bitcast(F32).rearrange("p i n -> p n i"))
-        nc.scalar.copy(out=w_woven[LO][:], in_=w_lo[:].rearrange("p i n -> p n i"))
+
+        def by_rows(t):
+            return t.rearrange("p i (c j) -> p c i j", j=LINE)
+
+        def woven(h):
+            return w_woven[:, h, :].rearrange("p (c j i) -> p c i j", j=LINE, i=PACK)
+
+        nc.gpsimd.tensor_tensor(
+            out=woven(LO), in0=by_rows(w_raw[:]), in1=by_rows(w_hi[:].bitcast(F32)), op=ALU.subtract,
+        )
+        nc.scalar.copy(out=woven(HI), in_=by_rows(w_hi[:].bitcast(F32)))
 
         nc.vector.tensor_copy(v_scales[:], scale_table[:].bitcast(U8).indirect(listed(0, S)))
-
-        w_scales = [
-            keep.tile([P, M], U8, name="hi_scales", tag="hi_buffer", align_bytes=64),
-            keep.tile([P, M], U8, name="lo_scales", align_bytes=64),
-        ]
-        codes_first = keep.tile([P, PIECE], U32, name="codes_first", tag="raw_buffer", align_bytes=64)
-        codes_rest = keep.tile([P, S - PIECE], U32, name="codes_rest", tag="lo_buffer", align_bytes=64)
-
-        def v_codes(a, b):
-            return codes_first[:, a:b] if b <= PIECE else codes_rest[:, a - PIECE : b - PIECE]
-
-        def quantize_w(h):
-            nc.vector.quantize_mx(
-                out=w_codes[h][:].bitcast(FP8X4), scales=w_scales[h][:],
-                in_=w_woven[h][:].rearrange("p n i -> p (n i)"),
-            )
-
-        def gather_words(a, b):
-            nc.vector.tensor_copy(v_codes(a, b), word_table[:].bitcast(U32).indirect(listed(a, b)))
-
+        nc.vector.quantize_mx(
+            out=w_codes[:].rearrange("p h n -> p (h n)").bitcast(FP8X4),
+            scales=w_scales[:].rearrange("p h n -> p (h n)"),
+            in_=w_woven[:].rearrange("p h c -> p (h c)"),
+        )
+        v_codes = keep.tile([P, S], U32, name="v_codes", tag="raw_buffer", align_bytes=64)
         pieces = spans([PIECE] * (S // PIECE))
-        quantize_w(HI)
-        gather_words(*pieces[0])
-        quantize_w(LO)
-        for a, b in pieces[1:]:
-            gather_words(a, b)
+        for a, b in pieces:
+            nc.vector.tensor_copy(v_codes[:, a:b], word_table[:].bitcast(U32).indirect(listed(a, b)))
 
         for a, b in pieces:
             acc = psum.tile([M, PIECE], F32, name="acc%d" % (a // PIECE))
             for h in (HI, LO):
                 nc.tensor.matmul_mx(
                     out=acc[:],
-                    lhsT=w_codes[h][:].bitcast(FP8X4),
-                    lhsT_scale=w_scales[h][:],
-                    rhs=v_codes(a, b).bitcast(FP8X4),
+                    lhsT=w_codes[:, h, :].bitcast(FP8X4),
+                    lhsT_scale=w_scales[:, h, :],
+                    rhs=v_codes[:, a:b].bitcast(FP8X4),
                     rhs_scale=v_scales[:, a:b],
                     start=(h == HI),
                     stop=(h == LO),

@@ -20,6 +20,7 @@ GROUP = 16
 QUADRANT = 32
 HI_MASK = -(1 << 20)
 HI, LO = 0, 1
+VECTOR_STRIPE, GPSIMD_STRIPE = 96, 112
 LINE = 4
 
 PIECE = 256
@@ -40,7 +41,8 @@ def tile_list_tabgate_none_kernel(tc, tab_words, tab_scales, w, gT, offs, out):
         psum = ctx.enter_context(tc.psum_pool(name="psum", bufs=1))
 
         offsets = keep.tile([P, S // GROUP], U16, name="offsets")
-        scale_table = keep.tile([P, T // 4], I32, name="scale_table", align_bytes=64)
+        scale_stripes = keep.tile([P, 3, VECTOR_STRIPE + GPSIMD_STRIPE], I32, name="scale_stripes", align_bytes=64)
+        scale_table = scale_stripes[:].rearrange("p s c -> p (s c)")[:, : T // 4]
         word_table = keep.tile([P, T], I32, name="word_table", align_bytes=64)
         gate_table = keep.tile([P, T], F32, name="gate_table", align_bytes=64)
         w_raw = keep.tile([P, PACK, M], F32, name="w_raw", tag="raw_buffer", align_bytes=64)
@@ -55,7 +57,8 @@ def tile_list_tabgate_none_kernel(tc, tab_words, tab_scales, w, gT, offs, out):
         def listed(a, b):
             return offsets[:, a // GROUP : b // GROUP]
 
-        nc.vector.memset(scale_table[:], 0)
+        nc.vector.memset(scale_stripes[:, :, :VECTOR_STRIPE], 0)
+        nc.gpsimd.memset(scale_stripes[:, :2, VECTOR_STRIPE:], 0)
         nc.sync.dma_start(out=w_raw[:], in_=w.rearrange("(p i) n -> p i n", i=PACK))
         nc.sync.dma_start(offsets[:], offs)
         scale_rows = tab_scales[0].bitcast(I32)
@@ -82,7 +85,7 @@ def tile_list_tabgate_none_kernel(tc, tab_words, tab_scales, w, gT, offs, out):
         )
         nc.scalar.copy(out=woven(HI), in_=by_rows(w_hi[:].bitcast(F32)))
 
-        nc.vector.tensor_copy(v_scales[:], scale_table[:].bitcast(U8).indirect(listed(0, S)))
+        nc.vector.tensor_copy(v_scales[:], scale_table.bitcast(U8).indirect(listed(0, S)))
         nc.vector.quantize_mx(
             out=w_codes[:].rearrange("p h n -> p (h n)").bitcast(FP8X4),
             scales=w_scales[:].rearrange("p h n -> p (h n)"),

@@ -20,6 +20,7 @@ GROUP = 16
 QUADRANT = 32
 HI_MASK = -(1 << 20)
 HI, LO = 0, 1
+PLANE_ROW = 12
 VECTOR_STRIPE, GPSIMD_STRIPE = 96, 112
 LINE = 4
 
@@ -63,7 +64,7 @@ def tile_list_tabgate_none_kernel(tc, tab_words, tab_scales, w, gT, offs, out):
         nc.sync.dma_start(offsets[:], offs)
         scale_rows = tab_scales[0].bitcast(I32)
         for r in range(4):
-            nc.sync.dma_start(out=scale_table[r:P:QUADRANT, :], in_=scale_rows[r:16:4, :])
+            nc.sync.dma_start(out=scale_table[PLANE_ROW + r : P : QUADRANT, :], in_=scale_rows[r:16:4, :])
         words = tab_words[0].rearrange("p t i -> p (t i)").bitcast(I32)
         for a, b in spans(WORD_LOADS):
             nc.sync.dma_start(out=word_table[:, a:b], in_=words[:, a:b])
@@ -104,7 +105,7 @@ def tile_list_tabgate_none_kernel(tc, tab_words, tab_scales, w, gT, offs, out):
                     lhsT=w_codes[:, h, :].bitcast(FP8X4),
                     lhsT_scale=w_scales[:, h, :],
                     rhs=v_codes[:, a:b].bitcast(FP8X4),
-                    rhs_scale=v_scales[:, a:b],
+                    rhs_scale=v_scales[PLANE_ROW:, a:b],
                     start=(h == HI),
                     stop=(h == LO),
                 )

from contextlib import ExitStack

import concourse.mybir as mybir

K, M, T, S = 512, 128, 2048, 1024
FLOPS = 2 * 2 * K * M * S

F32 = mybir.dt.float32
BF16 = mybir.dt.bfloat16
I32 = mybir.dt.int32
U32 = mybir.dt.uint32
U16 = mybir.dt.uint16
U8 = mybir.dt.uint8
FP8X4 = mybir.dt.float8_e4m3fn_x4
ALU = mybir.AluOpType

P = 128
PACK = 4
GROUP = 16
QUADRANT = 32
HI_MASK = -(1 << 20)
HI, LO = 0, 1
PLANE_ROW = 12
VECTOR_STRIPE, GPSIMD_STRIPE = 96, 112
LINE = 4

PIECE = 256
GATE_CUTS = [PIECE, PIECE, PIECE, PIECE // 2, PIECE // 2]
WORD_LOADS = [T // 2, T // 2]
GATE_LOADS = [T // 2, T // 4, T // 4]


def spans(widths):
    starts = [sum(widths[:i]) for i in range(len(widths))]
    return [(a, a + n) for a, n in zip(starts, widths)]


def tile_list_tabgate_none_kernel(tc, tab_words, tab_scales, w, gT, offs, out):
    nc = tc.nc
    with ExitStack() as ctx:
        keep = ctx.enter_context(tc.tile_pool(name="keep", bufs=1))
        psum = ctx.enter_context(tc.psum_pool(name="psum", bufs=1))

        offsets = keep.tile([P, S // GROUP], U16, name="offsets")
        scale_stripes = keep.tile([P, 3, VECTOR_STRIPE + GPSIMD_STRIPE], I32, name="scale_stripes", align_bytes=64)
        scale_table = scale_stripes[:].rearrange("p s c -> p (s c)")[:, : T // 4]
        word_table = keep.tile([P, T], I32, name="word_table", align_bytes=64)
        gate_table = keep.tile([P, T], F32, name="gate_table", align_bytes=64)
        w_raw = keep.tile([P, PACK, M], F32, name="w_raw", tag="raw_buffer", align_bytes=64)
        w_hi = keep.tile([P, PACK, M], I32, name="w_hi", align_bytes=64)
        w_woven = keep.tile([P, 2, M * PACK], BF16, name="w_woven", align_bytes=64)
        w_codes = keep.tile([P, 2, M], U32, name="w_codes", align_bytes=64)
        w_scales = keep.tile([P, 2, M], U8, name="w_scales", align_bytes=64)
        v_scales = keep.tile([P, S], U8, name="v_scales", align_bytes=64)
        y = keep.tile([P, S], F32, name="y", align_bytes=64)
        gated = keep.tile([P, S], F32, name="gated", align_bytes=64)

        def listed(a, b):
            return offsets[:, a // GROUP : b // GROUP]

        nc.vector.memset(scale_stripes[:, :, :VECTOR_STRIPE], 0)
        nc.gpsimd.memset(scale_stripes[:, :2, VECTOR_STRIPE:], 0)
        nc.sync.dma_start(out=w_raw[:], in_=w.rearrange("(p i) n -> p i n", i=PACK))
        nc.sync.dma_start(offsets[:], offs)
        scale_rows = tab_scales[0].bitcast(I32)
        for r in range(4):
            nc.sync.dma_start(out=scale_table[PLANE_ROW + r : P : QUADRANT, :], in_=scale_rows[r:16:4, :])
        words = tab_words[0].rearrange("p t i -> p (t i)").bitcast(I32)
        for a, b in spans(WORD_LOADS):
            nc.sync.dma_start(out=word_table[:, a:b], in_=words[:, a:b])
        for a, b in spans(GATE_LOADS):
            nc.sync.dma_start(out=gate_table[:, a:b], in_=gT[:, a:b])

        nc.vector.tensor_scalar(
            out=w_hi[:], in0=w_raw[:].bitcast(I32), scalar1=HI_MASK, scalar2=None, op0=ALU.bitwise_and,
        )

        def by_rows(t):
            return t.rearrange("p i (c j) -> p c i j", j=LINE)

        def woven(h):
            return w_woven[:, h, :].rearrange("p (c j i) -> p c i j", j=LINE, i=PACK)

        nc.gpsimd.tensor_tensor(
            out=woven(LO), in0=by_rows(w_raw[:]), in1=by_rows(w_hi[:].bitcast(F32)), op=ALU.subtract,
        )
        nc.scalar.copy(out=woven(HI), in_=by_rows(w_hi[:].bitcast(F32)))

        nc.vector.tensor_copy(v_scales[:], scale_table.bitcast(U8).indirect(listed(0, S)))
        nc.vector.quantize_mx(
            out=w_codes[:].rearrange("p h n -> p (h n)").bitcast(FP8X4),
            scales=w_scales[:].rearrange("p h n -> p (h n)"),
            in_=w_woven[:].rearrange("p h c -> p (h c)"),
        )
        v_codes = keep.tile([P, S], U32, name="v_codes", tag="raw_buffer", align_bytes=64)
        pieces = spans([PIECE] * (S // PIECE))
        for a, b in pieces:
            nc.vector.tensor_copy(v_codes[:, a:b], word_table[:].bitcast(U32).indirect(listed(a, b)))

        for a, b in pieces:
            acc = psum.tile([M, PIECE], F32, name="acc%d" % (a // PIECE))
            for h in (HI, LO):
                nc.tensor.matmul_mx(
                    out=acc[:],
                    lhsT=w_codes[:, h, :].bitcast(FP8X4),
                    lhsT_scale=w_scales[:, h, :],
                    rhs=v_codes[:, a:b].bitcast(FP8X4),
                    rhs_scale=v_scales[PLANE_ROW:, a:b],
                    start=(h == HI),
                    stop=(h == LO),
                )
            nc.scalar.copy(out=y[:, a:b], in_=acc[:])

        for a, b in spans(GATE_CUTS):
            nc.vector.tensor_tensor(gated[:, a:b], gate_table[:].indirect(listed(a, b)), y[:, a:b], ALU.mult)
            nc.sync.dma_start(out=out[:, a:b], in_=gated[:, a:b])
